import numpy as np
import ml_dtypes


def mxq(x, axis, fmt="e4m3"):
    dtype, down = {"e4m3": (ml_dtypes.float8_e4m3fn, 7), "e5m2": (ml_dtypes.float8_e5m2, 14)}[fmt]
    v = np.moveaxis(np.asarray(x, np.float32).astype(ml_dtypes.bfloat16).astype(np.float64), axis, -1)
    blocks = v.reshape(v.shape[:-1] + (-1, 32))
    amax = np.abs(blocks).max(-1, keepdims=True)
    byte = np.maximum(np.where(amax > 0, np.frexp(amax)[1] - 1 + 127, 0) - down, 1)
    scale = np.exp2(byte - 127.0)
    codes = (blocks / scale).astype(np.float32).astype(dtype).astype(np.float64)
    return np.moveaxis((codes * scale).reshape(v.shape), -1, axis)


WIDE = False


def mx_kscale(k):
    if not WIDE:
        return np.ones(k)
    levels = np.array([10, -10, 5, -5, 0])
    if k % 512:
        return np.exp2(np.random.permutation(np.resize(levels, k // 32))).repeat(32)
    a = np.empty((k // 512, 16))
    for p in range(k // 512):
        a[p, :8] = np.random.permutation(np.resize(levels, 8))
        for g in range(8):
            far = levels[np.abs(levels - a[p, g]) >= 10]
            a[p, g + 8] = far[np.random.randint(len(far))]
    return np.exp2(a.ravel()).repeat(32)


BF16 = ml_dtypes.bfloat16


def bf(x):
    return np.asarray(x, np.float32).astype(BF16)


def f64(x):
    return np.asarray(x).astype(np.float64)


E2M1 = np.array([0.0, 0.5, 1.0, 1.5, 2.0, 3.0, 4.0, 6.0, -0.0, -0.5, -1.0, -1.5, -2.0, -3.0, -4.0, -6.0])


def pack_weight(w, fmt):
    k, n = w.shape
    w = f64(bf(w)).reshape(k // 32, 32, n)
    amax = np.abs(w).max(1)
    if fmt == "e4m3":
        byte = np.frexp(amax)[1] - 1 + 127 - 7
    else:
        mant, ex = np.frexp(amax / 6.0)
        byte = np.where(mant > 0.5, ex, ex - 1) + 127
    byte = np.clip(np.where(amax > 0, byte, 1), 1, 254)
    scaled = (w * np.exp2(127.0 - byte)[:, None, :]).reshape(k, n).astype(np.float32)
    by_word = np.ascontiguousarray(scaled.reshape(k // 512, 128, 4, n).transpose(0, 1, 3, 2))
    if fmt == "e4m3":
        words = by_word.astype(ml_dtypes.float8_e4m3fn).view(np.uint8)
    else:
        c = by_word.astype(ml_dtypes.float4_e2m1fn).view(np.uint8) & 0xF
        words = c[..., 0::2] | (c[..., 1::2] << 4)
    return np.ascontiguousarray(words), np.ascontiguousarray(byte.astype(np.uint8).reshape(k // 512, 16, n))


def unpack_weight(words, scales, fmt):
    g, p, n, _ = words.shape
    if fmt == "e4m3":
        vals = np.ascontiguousarray(words).view(ml_dtypes.float8_e4m3fn).astype(np.float64)
    else:
        nib = np.empty((g, p, n, 4), np.uint8)
        nib[..., 0::2] = words & 0xF
        nib[..., 1::2] = words >> 4
        vals = E2M1[nib]
    vals = vals * np.repeat(np.exp2(scales.astype(np.float64) - 127.0), 8, axis=1)[..., None]
    return vals.transpose(0, 1, 3, 2).reshape(g * 512, n)
def pack4(w):
    words, scales = pack_weight(w, "e2m1")
    return words.reshape(words.shape[0], 128, -1), scales


def unpack4(words, scales):
    return unpack_weight(words.reshape(words.shape[0], 128, -1, 2), scales, "e2m1")


M, D, E, N, P = 1024, 1024, 512, 2048, 512


def setup_inputs():
    u, v, w = mx_kscale(D), mx_kscale(E), mx_kscale(N)
    a = np.sqrt(0.5) / D ** 0.25
    x1 = np.random.standard_normal((M, D)) * a
    z1 = np.random.standard_normal((D, N)) * a
    hx = 0.5 * np.sum(x1 * x1, axis=1)
    hz = 0.5 * np.sum(z1 * z1, axis=0)
    x2 = np.random.standard_normal((M, E))
    z2 = np.random.standard_normal((E, N)) * 0.5 / np.sqrt(E)
    alpha = np.random.standard_normal((N, P)) / np.sqrt(N)
    z1_words, z1_scales = pack4(z1 / u[:, None])
    z2_words, z2_scales = pack4(z2 / v[:, None])
    alpha_words, alpha_scales = pack_weight(alpha / w[:, None], "e4m3")
    return {"x1": bf(x1 * u),
            "x2": bf(x2 * v),
            "z1_words": z1_words, "z1_scales": z1_scales,
            "z2_words": z2_words, "z2_scales": z2_scales,
            "alpha_words": alpha_words, "alpha_scales": alpha_scales,
            "lx": bf(hx - hx.mean()),
            "lz": bf(hz - hz.mean()),
            "amp": bf((1 + 0.1 * np.random.standard_normal(N)) * w),
            "gain": bf(1 + 0.1 * np.random.standard_normal(P)),
            "prior": bf(0.3 * np.random.standard_normal(P))}


def reference(x1, x2, z1_words, z1_scales, z2_words, z2_scales, alpha_words, alpha_scales, lx, lz, amp, gain, prior):
    g1 = mxq(f64(x1), 1, "e4m3") @ unpack4(z1_words, z1_scales)
    g2 = mxq(f64(x2), 1, "e4m3") @ unpack4(z2_words, z2_scales)
    rbf = np.exp(g1 - f64(lx)[:, None] - f64(lz)[None, :])
    poly = np.square(1 + g2)
    kern = rbf * poly * f64(amp)[None, :]
    f = mxq(kern, 1, "e4m3") @ unpack_weight(alpha_words, alpha_scales, "e4m3")
    return f64(prior)[None, :] + f64(gain)[None, :] * f

@@ -1,0 +1,383 @@
+from contextlib import ExitStack
+
+import concourse.mybir as mybir
+from concourse.masks import make_identity
+
+M, D, E, N, C = 1024, 1024, 512, 2048, 512
+FLOPS = 2 * M * N * (D + E) + 2 * M * N * C
+
+F32 = mybir.dt.float32
+BF16 = mybir.dt.bfloat16
+I32 = mybir.dt.int32
+U32 = mybir.dt.uint32
+U8 = mybir.dt.uint8
+FP8X4 = mybir.dt.float8_e4m3fn_x4
+FP4X4 = mybir.dt.float4_e2m1fn_x4
+ALU = mybir.AluOpType
+ACT = mybir.ActivationFunctionType
+
+P = 128
+PACK = 4
+W = 512
+HALVES = M // W
+GROUPS = N // W
+TILES = HALVES * GROUPS * PACK
+Z_PASSES = 3
+C_TILES = C // P
+SCALAR_COLS = [320, 320, 320, 128, 128, 64, 128, 160]
+
+
+def tile_gp_product_kernel_mean_f7_kernel(
+    tc, x1, x2, z1_words, z1_scales, z2_words, z2_scales, alpha_words, alpha_scales, lx, lz, amp, gain, prior, out
+):
+    nc = tc.nc
+    with ExitStack() as ctx:
+        keep = ctx.enter_context(tc.tile_pool(name="keep", bufs=1))
+        work = ctx.enter_context(tc.tile_pool(name="work", bufs=2))
+        psum = ctx.enter_context(tc.psum_pool(name="psum", bufs=1))
+        ctx.enter_context(tc.manual_schedule())
+
+        ident = keep.tile([P, P], F32, name="ident")
+        warm = keep.tile([P, 1], F32, name="warm")
+        warm_out = keep.tile([P, 1], F32, name="warm_out")
+        z_raw = keep.tile([P, Z_PASSES, 2 * N], U8, name="z_raw", align_bytes=64)
+        zs_raw = keep.tile([P, Z_PASSES, W], U8, name="zs_raw", align_bytes=64)
+        zs_ordered = keep.tile([P, Z_PASSES * W], U8, name="zs_ordered", align_bytes=64)
+        z_codes = [keep.tile([P, Z_PASSES, 2 * W], U8, name="z_codes%d" % g, align_bytes=64) for g in range(GROUPS)]
+        z_scales = keep.tile([P, GROUPS, Z_PASSES * W], U8, name="z_scales", align_bytes=64)
+        a_codes = keep.tile([P, GROUPS, C], U32, name="a_codes", align_bytes=64)
+        a_scales = keep.tile([P, GROUPS, C], U8, name="a_scales", align_bytes=64)
+        x_rows = [
+            [keep.tile([P, PACK, W], BF16, name="x_rows%d_%d" % (h, a), align_bytes=64) for a in range(Z_PASSES)]
+            for h in range(HALVES)
+        ]
+        x_codes = [
+            [keep.tile([P, W], U32, name="x_codes%d_%d" % (h, a), align_bytes=64) for a in range(Z_PASSES)]
+            for h in range(HALVES)
+        ]
+        x_scales = [
+            [keep.tile([P, W], U8, name="x_scales%d_%d" % (h, a), align_bytes=64) for a in range(Z_PASSES)]
+            for h in range(HALVES)
+        ]
+        c_codes = [keep.tile([P, W], U32, name="c_codes%d" % u, align_bytes=64) for u in range(HALVES * GROUPS)]
+        c_scales = [keep.tile([P, W], U8, name="c_scales%d" % u, align_bytes=64) for u in range(HALVES * GROUPS)]
+        lx_all = [keep.tile([P, W], BF16, name="lx_all%d" % h) for h in range(HALVES)]
+        lz_raw = keep.tile([P, GROUPS, PACK], BF16, name="lz_raw")
+        amp_raw = keep.tile([P, GROUPS, PACK], BF16, name="amp_raw")
+        lz_col = keep.tile([P, GROUPS * PACK], F32, name="lz_col")
+        amp_col = keep.tile([P, GROUPS * PACK], F32, name="amp_col")
+        gain_raw = keep.tile([P, C_TILES, 2], BF16, name="gain_raw")
+        prior_raw = keep.tile([P, C_TILES, 2], BF16, name="prior_raw")
+        gain_col = keep.tile([P, C_TILES], F32, name="gain_col")
+        prior_col = keep.tile([P, C_TILES], F32, name="prior_col")
+
+        def bank(tag, bufs=1):
+            return psum.tile([P, W], F32, name=tag, tag=tag, bufs=bufs)
+
+        def spare_bank(b):
+            return bank("spare%d" % b)
+
+        def load_z_codes(cols):
+            nc.sync.dma_start(
+                out=z_raw[:, 0:2, cols].bitcast(I32), in_=z1_words[:, :, cols].rearrange("g p n -> p g n").bitcast(I32)
+            )
+            nc.sync.dma_start(out=z_raw[:, 2, cols].bitcast(I32), in_=z2_words[0, :, cols].bitcast(I32))
+
+        def load_x(h, a):
+            src = x1[:, a * W : (a + 1) * W] if a < 2 else x2
+            nc.sync.dma_start(out=x_rows[h][a][:], in_=src[h * W : (h + 1) * W, :].rearrange("(c p) k -> p c k", p=P))
+
+        def load_scale_rows(queue, plane, rows):
+            for q in range(4):
+                queue.dma_start(
+                    out=plane[32 * q : 32 * q + 4].bitcast(I32),
+                    in_=rows[:, 4 * q : 4 * q + 4, :].rearrange("g r n -> r g n").bitcast(I32),
+                )
+
+        def order_z_codes(g, a):
+            nc.vector.tensor_copy(
+                out=z_codes[g][:, a, :].rearrange("p (t m b) -> p t m b", t=PACK, b=2),
+                in_=z_raw[:, a, 2 * W * g : 2 * W * (g + 1)].rearrange("p (m t b) -> p t m b", t=PACK, b=2),
+            )
+
+        def order_z_scales():
+            nc.vector.tensor_copy(
+                out=zs_ordered[:].rearrange("p (a t m) -> p t a m", a=Z_PASSES, t=PACK),
+                in_=zs_raw[:].rearrange("p a (m t) -> p t a m", t=PACK),
+            )
+
+        def place_z_scales(queue, g):
+            for q in range(4):
+                queue.dma_start(
+                    out=z_scales[32 * q : 32 * q + 4, g, :].bitcast(I32),
+                    in_=zs_ordered[16 * q + g : 16 * (q + 1) : 4, :].bitcast(I32),
+                )
+
+        x_banks = {}
+        x_grouped = {}
+
+        def turn_x(h, a, pair):
+            xt = spare_bank((2 * a + pair) % 4)
+            x_banks[(h, a, pair)] = xt
+            for c in range(2):
+                words = x_rows[h][a][:, 2 * pair + c, :].bitcast(F32)
+                for u in range(2):
+                    col = (2 * c + u) * P
+                    nc.tensor.transpose(xt[:, col : col + P], words[:, u : W // 2 : 2], ident[:])
+
+        def group_x(h, a, pair, on_vector=False):
+            if pair == 0:
+                x_grouped[(h, a)] = work.tile([P, PACK * W], BF16, name="x_grouped", align_bytes=64, bufs=3)
+            dst = x_grouped[(h, a)][:].bitcast(F32)[:, pair * W : (pair + 1) * W]
+            dst = dst.rearrange("p (c r u) -> p c r u", c=2, u=2)
+            src = x_banks[(h, a, pair)][:].rearrange("p (c u r) -> p c r u", c=2, u=2)
+            if on_vector:
+                nc.vector.tensor_copy(out=dst, in_=src)
+            else:
+                nc.scalar.copy(out=dst, in_=src)
+
+        def quantize_x(h, a):
+            nc.vector.quantize_mx(
+                out=x_codes[h][a][:].bitcast(FP8X4), scales=x_scales[h][a][:], in_=x_grouped[(h, a)][:]
+            )
+
+        g1, g2, arg, rbf, poly, kern, kern_grouped = {}, {}, {}, {}, {}, {}, {}
+
+        def products(k):
+            h, g, t = k // (GROUPS * PACK), k // PACK % GROUPS, k % PACK
+            g1[k] = bank("g1", 2)
+            g2[k] = bank("g2", 2)
+            for a in range(Z_PASSES):
+                nc.tensor.matmul_mx(
+                    out=(g1[k] if a < 2 else g2[k])[:],
+                    lhsT=z_codes[g][:, a, 2 * P * t : 2 * P * (t + 1)].bitcast(FP4X4),
+                    lhsT_scale=z_scales[:, g, W * a + P * t : W * a + P * (t + 1)],
+                    rhs=x_codes[h][a][:].bitcast(FP8X4),
+                    rhs_scale=x_scales[h][a][:],
+                    start=(a != 1),
+                    stop=(a != 0),
+                )
+
+        def exponent(k):
+            j = k % (GROUPS * PACK)
+            arg[k] = work.tile([P, W], F32, name="arg", bufs=3)
+            nc.vector.scalar_tensor_tensor(
+                out=arg[k][:],
+                in0=g1[k][:],
+                scalar=lz_col[:, j : j + 1],
+                in1=lx_all[k // (GROUPS * PACK)][:],
+                op0=ALU.subtract,
+                op1=ALU.subtract,
+            )
+
+        def exponential(k):
+            rbf[k] = work.tile([P, W], F32, name="rbf", bufs=3)
+            nc.scalar.activation(out=rbf[k][:], in_=arg[k][:], func=ACT.Exp)
+
+        def square(k):
+            poly[k] = work.tile([P, W], F32, name="poly", bufs=4)
+            nc.scalar.activation(out=poly[k][:], in_=g2[k][:], func=ACT.Square, bias=1.0)
+
+        def kernel_values(k):
+            j = k % (GROUPS * PACK)
+            if k % PACK == 0:
+                kern[k // PACK] = work.tile([P, PACK, W], BF16, name="kern", align_bytes=64)
+            nc.vector.scalar_tensor_tensor(
+                out=kern[k // PACK][:, k % PACK, :],
+                in0=rbf[k][:],
+                scalar=amp_col[:, j : j + 1],
+                in1=poly[k][:],
+                op0=ALU.mult,
+                op1=ALU.mult,
+            )
+
+        def group_kernel(u, lo, hi, on_vector):
+            if u not in kern_grouped:
+                kern_grouped[u] = work.tile([P, W, PACK], BF16, name="kern_grouped", align_bytes=64)
+            dst = kern_grouped[u][:, lo:hi, :].rearrange("p (c i) t -> p c t i", i=4)
+            src = kern[u][:, :, lo:hi].rearrange("p t (c i) -> p c t i", i=4)
+            if on_vector:
+                nc.vector.tensor_copy(out=dst, in_=src)
+            else:
+                nc.scalar.copy(out=dst, in_=src)
+
+        def quantize_kernel(u):
+            nc.vector.quantize_mx(
+                out=c_codes[u][:].bitcast(FP8X4),
+                scales=c_scales[u][:],
+                in_=kern_grouped[u][:].rearrange("p i t -> p (i t)"),
+            )
+
+        f_banks, means, turned = {}, {}, {}
+
+        def mean_passes(h, c, groups):
+            for g in groups:
+                if g == 0:
+                    f_banks[(h, c)] = spare_bank(c % 2 if h == 0 else c)
+                nc.tensor.matmul_mx(
+                    out=f_banks[(h, c)][:],
+                    lhsT=a_codes[:, g, P * c : P * (c + 1)].bitcast(FP8X4),
+                    lhsT_scale=a_scales[:, g, P * c : P * (c + 1)],
+                    rhs=c_codes[h * GROUPS + g][:].bitcast(FP8X4),
+                    rhs_scale=c_scales[h * GROUPS + g][:],
+                    start=(g == 0),
+                    stop=(g == GROUPS - 1),
+                )
+
+        def rescale(h, c, on_vector=False):
+            means[(h, c)] = work.tile([P, W], F32, name="means", bufs=4)
+            if on_vector:
+                nc.vector.tensor_scalar(
+                    out=means[(h, c)][:],
+                    in0=f_banks[(h, c)][:],
+                    scalar1=gain_col[:, c : c + 1],
+                    scalar2=prior_col[:, c : c + 1],
+                    op0=ALU.mult,
+                    op1=ALU.add,
+                )
+            else:
+                nc.scalar.activation(
+                    out=means[(h, c)][:],
+                    in_=f_banks[(h, c)][:],
+                    func=ACT.Identity,
+                    scale=gain_col[:, c : c + 1],
+                    bias=prior_col[:, c : c + 1],
+                )
+
+        def turn_mean(h, c):
+            turned[(h, c)] = spare_bank(2 + c % 2) if h == 0 else bank("g1" if c % 2 == 0 else "g2", 2)
+            for r in range(W // P):
+                cols = slice(P * r, P * (r + 1))
+                nc.tensor.transpose(turned[(h, c)][:, cols], means[(h, c)][:, cols], ident[:])
+
+        def store_mean(h, c, on_vector=False):
+            rows = work.tile([P, W], F32, name="rows", bufs=4)
+            if on_vector:
+                nc.vector.tensor_copy(out=rows[:], in_=turned[(h, c)][:])
+            else:
+                nc.scalar.copy(out=rows[:], in_=turned[(h, c)][:])
+            nc.sync.dma_start(
+                out=out[h * W : (h + 1) * W, P * c : P * (c + 1)].rearrange("(r p) c -> p r c", p=P),
+                in_=rows[:].rearrange("p (r c) -> p r c", c=P),
+            )
+
+        nc.vector.memset(warm[:], 0.0)
+        nc.vector.memset(zs_raw[64:P].rearrange("p a n -> p (a n)").bitcast(I32), 0)
+        nc.vector.memset(z_scales[:].rearrange("p g n -> p (g n)").bitcast(I32), 0)
+        nc.vector.memset(a_scales[:].rearrange("p g n -> p (g n)").bitcast(I32), 0)
+        make_identity(nc, ident[:])
+        nc.sync.dma_start(
+            out=zs_raw[0:64, 0:2, :].bitcast(I32), in_=z1_scales.rearrange("a q (g m) -> (q g) a m", m=W).bitcast(I32)
+        )
+        nc.sync.dma_start(
+            out=zs_raw[0:64, 2, :].bitcast(I32), in_=z2_scales[0].rearrange("q (g m) -> (q g) m", m=W).bitcast(I32)
+        )
+        load_x(0, 0)
+        load_z_codes(slice(0, 2 * W))
+        load_x(0, 1)
+        load_x(0, 2)
+        nc.scalar.dma_start(out=lz_raw[:], in_=lz.rearrange("(g p t) -> p g t", p=P, t=PACK))
+        nc.scalar.activation(out=warm_out[:], in_=warm[:], func=ACT.Exp)
+        order_z_scales()
+        place_z_scales(nc.sync, 0)
+        nc.sync.dma_start(out=lx_all[0][:], in_=lx[0:W].partition_broadcast(P))
+        nc.sync.dma_start(out=amp_raw[:], in_=amp.rearrange("(g p t) -> p g t", p=P, t=PACK))
+        nc.gpsimd.tensor_copy(out=lz_col[:], in_=lz_raw[:].rearrange("p g t -> p (g t)"))
+        nc.gpsimd.tensor_copy(out=amp_col[:], in_=amp_raw[:].rearrange("p g t -> p (g t)"))
+        load_z_codes(slice(2 * W, 4 * W))
+        place_z_scales(nc.sync, 1)
+        load_z_codes(slice(4 * W, 2 * N))
+        for g in range(2, GROUPS):
+            place_z_scales(nc.sync, g)
+        for a in range(Z_PASSES):
+            load_x(1, a)
+        nc.sync.dma_start(out=lx_all[1][:], in_=lx[W : 2 * W].partition_broadcast(P))
+        nc.sync.dma_start(
+            out=a_codes[:].bitcast(I32), in_=alpha_words.rearrange("g p n t -> p g (n t)").bitcast(I32)
+        )
+        load_scale_rows(nc.sync, a_scales, alpha_scales)
+        nc.sync.dma_start(
+            out=gain_raw[:, :, 0], in_=gain.rearrange("(c p) -> p c", p=P), allow_slow_non_contiguous=True
+        )
+        nc.sync.dma_start(
+            out=prior_raw[:, :, 0], in_=prior.rearrange("(c p) -> p c", p=P), allow_slow_non_contiguous=True
+        )
+
+        for a in range(Z_PASSES):
+            turn_x(0, a, 0)
+            turn_x(0, a, 1)
+            group_x(0, a, 0)
+            group_x(0, a, 1)
+        order_z_codes(0, 0)
+        order_z_codes(0, 1)
+        quantize_x(0, 0)
+        order_z_codes(0, 2)
+        quantize_x(0, 1)
+        order_z_codes(1, 0)
+        quantize_x(0, 2)
+        products(0)
+
+        tensor_extra, scalar_extra, vector_extra = {}, {}, {}
+
+        def at(table, step, fn, *args):
+            table.setdefault(step, []).append((fn, args))
+
+        for g in range(1, GROUPS):
+            for a in range(Z_PASSES):
+                if (g, a) != (1, 0):
+                    at(vector_extra, 4 * g - 5 + a, order_z_codes, g, a)
+        for a in range(Z_PASSES):
+            for pair in range(2):
+                step = 1 + 4 * a + 2 * pair
+                at(tensor_extra, step, turn_x, 1, a, pair)
+                at(scalar_extra, step + 1, group_x, 1, a, pair)
+            at(vector_extra, 6 + 4 * a, quantize_x, 1, a)
+        last = HALVES * GROUPS - 1
+        for u in range(last):
+            split = W - SCALAR_COLS[u]
+            mid = split + SCALAR_COLS[u] // 2
+            at(vector_extra, 4 * u + 6, group_kernel, u, 0, split, True)
+            at(scalar_extra, 4 * u + 6, group_kernel, u, split, mid, False)
+            at(scalar_extra, 4 * u + 7, group_kernel, u, mid, W, False)
+            at(vector_extra, 4 * u + 8, quantize_kernel, u)
+        at(vector_extra, 16, nc.vector.tensor_copy, gain_col[:], gain_raw[:, :, 0])
+        at(vector_extra, 16, nc.vector.tensor_copy, prior_col[:], prior_raw[:, :, 0])
+        for c in range(C_TILES):
+            at(tensor_extra, 21 + 2 * c, mean_passes, 0, c, range(GROUPS))
+            at(scalar_extra, 22 + 2 * c, rescale, 0, c)
+            at(tensor_extra, 23 + 2 * c, turn_mean, 0, c)
+            at(scalar_extra, 24 + 2 * c, store_mean, 0, c)
+        for c, step in enumerate((29, 29, 30, 31)):
+            at(tensor_extra, step, mean_passes, 1, c, range(2))
+        for c in range(C_TILES):
+            at(tensor_extra, 33, mean_passes, 1, c, range(2, 3))
+
+        for s in range(TILES + 2):
+            if s + 1 < TILES:
+                products(s + 1)
+            for fn, args in tensor_extra.get(s, []):
+                fn(*args)
+            if 1 <= s <= TILES:
+                exponential(s - 1)
+            if s < TILES:
+                square(s)
+                exponent(s)
+            for fn, args in vector_extra.get(s, []):
+                fn(*args)
+            for fn, args in scalar_extra.get(s, []):
+                fn(*args)
+            if s >= 2:
+                kernel_values(s - 2)
+
+        split = W - SCALAR_COLS[last]
+        group_kernel(last, split, W, False)
+        group_kernel(last, 0, split, True)
+        quantize_kernel(last)
+        for c in range(C_TILES):
+            mean_passes(1, c, range(GROUPS - 1, GROUPS))
+        for c in range(C_TILES):
+            rescale(1, c, on_vector=(c % 2 == 1))
+        for c in range(C_TILES):
+            turn_mean(1, c)
+        for c in range(C_TILES):
+            store_mean(1, c, on_vector=(c % 2 == 1))

@@ -19,12 +19,21 @@ ACT = mybir.ActivationFunctionType
 P = 128
 PACK = 4
 W = 512
-HALVES = M // W
+H = W // 2
 GROUPS = N // W
-TILES = HALVES * GROUPS * PACK
 Z_PASSES = 3
 C_TILES = C // P
-SCALAR_COLS = [320, 320, 320, 128, 128, 64, 128, 160]
+CHUNKS = ((0, H), (H, W), (H + W, H))
+STEPS = 16
+REST_ON = "ssfvxvvvssvsvvs"
+X_ON = "ssssssssv"
+EPI_A = "ssssss"
+EPI_B = "sssssvsv"
+Q_LATE = "000000000000000"
+X_STEPS = (1, 1, 2, 2, 3, 3, 4, 5, 9)
+G_COLS = (160, 160, 160, 160, 160, 160, 160, 160, 160, 160, 160, 160, 160, 160, 160)
+FULL_ON = "vs"
+TAIL_SPLIT = 176
 
 
 def tile_gp_product_kernel_mean_f7_kernel(
@@ -40,28 +49,26 @@ def tile_gp_product_kernel_mean_f7_kernel(
         ident = keep.tile([P, P], F32, name="ident")
         warm = keep.tile([P, 1], F32, name="warm")
         warm_out = keep.tile([P, 1], F32, name="warm_out")
-        z_raw = keep.tile([P, Z_PASSES, 2 * N], U8, name="z_raw", align_bytes=64)
+        z_parts = [
+            keep.tile([P, Z_PASSES, 2 * W * n], U8, name="z_part%d" % g, align_bytes=64) for g, n in enumerate((1, 1, 2))
+        ]
+        z_raw = [z_parts[0][:], z_parts[1][:], z_parts[2][:, :, 0 : 2 * W], z_parts[2][:, :, 2 * W : 4 * W]]
         zs_raw = keep.tile([P, Z_PASSES, W], U8, name="zs_raw", align_bytes=64)
         zs_ordered = keep.tile([P, Z_PASSES * W], U8, name="zs_ordered", align_bytes=64)
         z_codes = [keep.tile([P, Z_PASSES, 2 * W], U8, name="z_codes%d" % g, align_bytes=64) for g in range(GROUPS)]
         z_scales = keep.tile([P, GROUPS, Z_PASSES * W], U8, name="z_scales", align_bytes=64)
         a_codes = keep.tile([P, GROUPS, C], U32, name="a_codes", align_bytes=64)
         a_scales = keep.tile([P, GROUPS, C], U8, name="a_scales", align_bytes=64)
-        x_rows = [
-            [keep.tile([P, PACK, W], BF16, name="x_rows%d_%d" % (h, a), align_bytes=64) for a in range(Z_PASSES)]
-            for h in range(HALVES)
-        ]
-        x_codes = [
-            [keep.tile([P, W], U32, name="x_codes%d_%d" % (h, a), align_bytes=64) for a in range(Z_PASSES)]
-            for h in range(HALVES)
-        ]
-        x_scales = [
-            [keep.tile([P, W], U8, name="x_scales%d_%d" % (h, a), align_bytes=64) for a in range(Z_PASSES)]
-            for h in range(HALVES)
-        ]
-        c_codes = [keep.tile([P, W], U32, name="c_codes%d" % u, align_bytes=64) for u in range(HALVES * GROUPS)]
-        c_scales = [keep.tile([P, W], U8, name="c_scales%d" % u, align_bytes=64) for u in range(HALVES * GROUPS)]
-        lx_all = [keep.tile([P, W], BF16, name="lx_all%d" % h) for h in range(HALVES)]
+        x_rows, x_codes, x_scales, c_codes, c_scales, lx_all = {}, {}, {}, {}, {}, {}
+        for h, (row0, width) in enumerate(CHUNKS):
+            lx_all[h] = keep.tile([P, width], BF16, name="lx_all%d" % h)
+            for a in range(Z_PASSES):
+                x_rows[(h, a)] = keep.tile([P, width // P, W], BF16, name="x_rows%d_%d" % (h, a), align_bytes=64)
+                x_codes[(h, a)] = keep.tile([P, width], U32, name="x_codes%d_%d" % (h, a), align_bytes=64)
+                x_scales[(h, a)] = keep.tile([P, width], U8, name="x_scales%d_%d" % (h, a), align_bytes=64)
+            for g in range(GROUPS):
+                c_codes[(h, g)] = keep.tile([P, width], U32, name="c_codes%d_%d" % (h, g), align_bytes=64)
+                c_scales[(h, g)] = keep.tile([P, width], U8, name="c_scales%d_%d" % (h, g), align_bytes=64)
         lz_raw = keep.tile([P, GROUPS, PACK], BF16, name="lz_raw")
         amp_raw = keep.tile([P, GROUPS, PACK], BF16, name="amp_raw")
         lz_col = keep.tile([P, GROUPS * PACK], F32, name="lz_col")
@@ -77,15 +84,23 @@ def tile_gp_product_kernel_mean_f7_kernel(
         def spare_bank(b):
             return bank("spare%d" % b)
 
-        def load_z_codes(cols):
+        def load_z_codes(g):
+            cols = slice(2 * W * g, 2 * W * g + z_parts[g].shape[2])
             nc.sync.dma_start(
-                out=z_raw[:, 0:2, cols].bitcast(I32), in_=z1_words[:, :, cols].rearrange("g p n -> p g n").bitcast(I32)
+                out=z_parts[g][:, 0:2, :].bitcast(I32), in_=z1_words[:, :, cols].rearrange("g p n -> p g n").bitcast(I32)
             )
-            nc.sync.dma_start(out=z_raw[:, 2, cols].bitcast(I32), in_=z2_words[0, :, cols].bitcast(I32))
+            nc.sync.dma_start(out=z_parts[g][:, 2, :].bitcast(I32), in_=z2_words[0, :, cols].bitcast(I32))
 
         def load_x(h, a):
+            row0, width = CHUNKS[h]
             src = x1[:, a * W : (a + 1) * W] if a < 2 else x2
-            nc.sync.dma_start(out=x_rows[h][a][:], in_=src[h * W : (h + 1) * W, :].rearrange("(c p) k -> p c k", p=P))
+            nc.sync.dma_start(
+                out=x_rows[(h, a)][:], in_=src[row0 : row0 + width, :].rearrange("(c p) k -> p c k", p=P)
+            )
+
+        def load_lx(h):
+            row0, width = CHUNKS[h]
+            nc.sync.dma_start(out=lx_all[h][:], in_=lx[row0 : row0 + width].partition_broadcast(P))
 
         def load_scale_rows(queue, plane, rows):
             for q in range(4):
@@ -97,7 +112,7 @@ def tile_gp_product_kernel_mean_f7_kernel(
         def order_z_codes(g, a):
             nc.vector.tensor_copy(
                 out=z_codes[g][:, a, :].rearrange("p (t m b) -> p t m b", t=PACK, b=2),
-                in_=z_raw[:, a, 2 * W * g : 2 * W * (g + 1)].rearrange("p (m t b) -> p t m b", t=PACK, b=2),
+                in_=z_raw[g][:, a, :].rearrange("p (m t b) -> p t m b", t=PACK, b=2),
             )
 
         def order_z_scales():
@@ -116,120 +131,174 @@ def tile_gp_product_kernel_mean_f7_kernel(
         x_banks = {}
         x_grouped = {}
 
-        def turn_x(h, a, pair):
-            xt = spare_bank((2 * a + pair) % 4)
+        def turn_x(h, a, pair, b):
+            xt = spare_bank(b)
             x_banks[(h, a, pair)] = xt
             for c in range(2):
-                words = x_rows[h][a][:, 2 * pair + c, :].bitcast(F32)
+                words = x_rows[(h, a)][:, 2 * pair + c, :].bitcast(F32)
                 for u in range(2):
                     col = (2 * c + u) * P
                     nc.tensor.transpose(xt[:, col : col + P], words[:, u : W // 2 : 2], ident[:])
 
-        def group_x(h, a, pair, on_vector=False):
-            if pair == 0:
-                x_grouped[(h, a)] = work.tile([P, PACK * W], BF16, name="x_grouped", align_bytes=64, bufs=3)
-            dst = x_grouped[(h, a)][:].bitcast(F32)[:, pair * W : (pair + 1) * W]
-            dst = dst.rearrange("p (c r u) -> p c r u", c=2, u=2)
-            src = x_banks[(h, a, pair)][:].rearrange("p (c u r) -> p c r u", c=2, u=2)
-            if on_vector:
+        def copy_out(engine, dst, src):
+            if engine == "v":
                 nc.vector.tensor_copy(out=dst, in_=src)
             else:
                 nc.scalar.copy(out=dst, in_=src)
+
+        def group_x(h, a, pair, engine):
+            if pair == 0:
+                x_grouped[(h, a)] = work.tile([P, PACK * CHUNKS[h][1]], BF16, name="x_grouped", align_bytes=64, bufs=3)
+            dst = x_grouped[(h, a)][:].bitcast(F32)[:, pair * W : (pair + 1) * W]
+            copy_out(
+                engine,
+                dst.rearrange("p (c r u) -> p c r u", c=2, u=2),
+                x_banks[(h, a, pair)][:].rearrange("p (c u r) -> p c r u", c=2, u=2),
+            )
 
         def quantize_x(h, a):
             nc.vector.quantize_mx(
-                out=x_codes[h][a][:].bitcast(FP8X4), scales=x_scales[h][a][:], in_=x_grouped[(h, a)][:]
+                out=x_codes[(h, a)][:].bitcast(FP8X4), scales=x_scales[(h, a)][:], in_=x_grouped[(h, a)][:]
             )
+
+        slots = []
+        for h, (row0, width) in enumerate(CHUNKS):
+            per_bank = W // width
+            for g in range(GROUPS):
+                for t in range(0, PACK, per_bank):
+                    slots.append((h, g, list(range(t, t + per_bank))))
 
         g1, g2, arg, rbf, poly, kern, kern_grouped = {}, {}, {}, {}, {}, {}, {}
 
-        def products(k):
-            h, g, t = k // (GROUPS * PACK), k // PACK % GROUPS, k % PACK
-            g1[k] = bank("g1", 2)
-            g2[k] = bank("g2", 2)
-            for a in range(Z_PASSES):
-                nc.tensor.matmul_mx(
-                    out=(g1[k] if a < 2 else g2[k])[:],
-                    lhsT=z_codes[g][:, a, 2 * P * t : 2 * P * (t + 1)].bitcast(FP4X4),
-                    lhsT_scale=z_scales[:, g, W * a + P * t : W * a + P * (t + 1)],
-                    rhs=x_codes[h][a][:].bitcast(FP8X4),
-                    rhs_scale=x_scales[h][a][:],
-                    start=(a != 1),
-                    stop=(a != 0),
-                )
-
-        def exponent(k):
-            j = k % (GROUPS * PACK)
-            arg[k] = work.tile([P, W], F32, name="arg", bufs=3)
-            nc.vector.scalar_tensor_tensor(
-                out=arg[k][:],
-                in0=g1[k][:],
-                scalar=lz_col[:, j : j + 1],
-                in1=lx_all[k // (GROUPS * PACK)][:],
-                op0=ALU.subtract,
-                op1=ALU.subtract,
+        def z_pass(dst, h, g, t, a, cols, start, stop):
+            nc.tensor.matmul_mx(
+                out=dst,
+                lhsT=z_codes[g][:, a, 2 * P * t : 2 * P * (t + 1)].bitcast(FP4X4),
+                lhsT_scale=z_scales[:, g, W * a + P * t : W * a + P * (t + 1)],
+                rhs=x_codes[(h, a)][:, cols].bitcast(FP8X4),
+                rhs_scale=x_scales[(h, a)][:, cols],
+                start=start,
+                stop=stop,
             )
 
+        def product_1(k):
+            h, g, ts = slots[k]
+            width = CHUNKS[h][1]
+            n = W if width == W else P
+            g1[k] = bank("g1", 2)
+            for place, t in enumerate(ts):
+                for lo in range(0, width, n):
+                    dst = g1[k][:, place * width + lo : place * width + lo + n]
+                    z_pass(dst, h, g, t, 0, slice(lo, lo + n), True, False)
+                    z_pass(dst, h, g, t, 1, slice(lo, lo + n), False, True)
+
+        def product_2(k):
+            h, g, ts = slots[k]
+            width = CHUNKS[h][1]
+            g2[k] = bank("g2", 2)
+            for place, t in enumerate(ts):
+                z_pass(g2[k][:, place * width : (place + 1) * width], h, g, t, 2, slice(0, width), True, True)
+
+        def exponent(k):
+            h, g, ts = slots[k]
+            width = CHUNKS[h][1]
+            arg[k] = work.tile([P, W], F32, name="arg", bufs=4)
+            for place, t in enumerate(ts):
+                cols = slice(place * width, (place + 1) * width)
+                nc.vector.scalar_tensor_tensor(
+                    out=arg[k][:, cols],
+                    in0=g1[k][:, cols],
+                    scalar=lz_col[:, PACK * g + t : PACK * g + t + 1],
+                    in1=lx_all[h][:],
+                    op0=ALU.subtract,
+                    op1=ALU.subtract,
+                )
+
         def exponential(k):
-            rbf[k] = work.tile([P, W], F32, name="rbf", bufs=3)
+            rbf[k] = work.tile([P, W], F32, name="rbf", bufs=4)
             nc.scalar.activation(out=rbf[k][:], in_=arg[k][:], func=ACT.Exp)
 
         def square(k):
-            poly[k] = work.tile([P, W], F32, name="poly", bufs=4)
+            h, g, ts = slots[k]
+            if h == 1 and g > 0 and ts[0] == 1:
+                poly[k] = work.tile([P, W], F32, name="paced", tag="paced%d" % (g % 2), align_bytes=64, bufs=1)
+            else:
+                poly[k] = work.tile([P, W], F32, name="poly", bufs=4)
             nc.scalar.activation(out=poly[k][:], in_=g2[k][:], func=ACT.Square, bias=1.0)
 
         def kernel_values(k):
-            j = k % (GROUPS * PACK)
-            if k % PACK == 0:
-                kern[k // PACK] = work.tile([P, PACK, W], BF16, name="kern", align_bytes=64)
-            nc.vector.scalar_tensor_tensor(
-                out=kern[k // PACK][:, k % PACK, :],
-                in0=rbf[k][:],
-                scalar=amp_col[:, j : j + 1],
-                in1=poly[k][:],
-                op0=ALU.mult,
-                op1=ALU.mult,
-            )
+            h, g, ts = slots[k]
+            width = CHUNKS[h][1]
+            if ts[0] == 0:
+                kern[(h, g)] = work.tile([P, PACK, width], BF16, name="kern", align_bytes=64, bufs=3)
+            for place, t in enumerate(ts):
+                cols = slice(place * width, (place + 1) * width)
+                nc.vector.scalar_tensor_tensor(
+                    out=kern[(h, g)][:, t, :],
+                    in0=rbf[k][:, cols],
+                    scalar=amp_col[:, PACK * g + t : PACK * g + t + 1],
+                    in1=poly[k][:, cols],
+                    op0=ALU.mult,
+                    op1=ALU.mult,
+                )
 
-        def group_kernel(u, lo, hi, on_vector):
-            if u not in kern_grouped:
-                kern_grouped[u] = work.tile([P, W, PACK], BF16, name="kern_grouped", align_bytes=64)
-            dst = kern_grouped[u][:, lo:hi, :].rearrange("p (c i) t -> p c t i", i=4)
-            src = kern[u][:, :, lo:hi].rearrange("p t (c i) -> p c t i", i=4)
-            if on_vector:
-                nc.vector.tensor_copy(out=dst, in_=src)
+        def group_kernel(h, g, half, lo, hi, engine):
+            if (h, g, half) not in kern_grouped:
+                if half == 1 and g < GROUPS - 1:
+                    tag = "paced%d" % ((g + 1) % 2)
+                else:
+                    tag = "kern_grouped%d_%d" % (half, g % 2)
+                kern_grouped[(h, g, half)] = work.tile(
+                    [P, H, PACK], BF16, name="kern_grouped", tag=tag, align_bytes=64, bufs=1
+                )
+            dst = kern_grouped[(h, g, half)][:, lo:hi, :]
+            src = kern[(h, g)][:, :, half * H + lo : half * H + hi]
+            if engine == "g":
+                nc.gpsimd.tensor_scalar(
+                    out=dst, in0=src.rearrange("p t i -> p i t"), scalar1=1.0, scalar2=0.0, op0=ALU.mult, op1=ALU.add
+                )
             else:
-                nc.scalar.copy(out=dst, in_=src)
+                copy_out(
+                    engine, dst.rearrange("p (c i) t -> p c t i", i=4), src.rearrange("p t (c i) -> p c t i", i=4)
+                )
 
-        def quantize_kernel(u):
+        def quantize_kernel(h, g, half):
+            cols = slice(half * H, (half + 1) * H)
             nc.vector.quantize_mx(
-                out=c_codes[u][:].bitcast(FP8X4),
-                scales=c_scales[u][:],
-                in_=kern_grouped[u][:].rearrange("p i t -> p (i t)"),
+                out=c_codes[(h, g)][:, cols].bitcast(FP8X4),
+                scales=c_scales[(h, g)][:, cols],
+                in_=kern_grouped[(h, g, half)][:].rearrange("p i t -> p (i t)"),
             )
 
-        f_banks, means, turned = {}, {}, {}
+        f_sums, means, turned = {}, {}, {}
 
         def mean_passes(h, c, groups):
             for g in groups:
                 if g == 0:
-                    f_banks[(h, c)] = spare_bank(c % 2 if h == 0 else c)
+                    if h == 0:
+                        if c % 2 == 0:
+                            f_sums[(h, "bank")] = spare_bank(c // 2)
+                        f_sums[(h, c)] = f_sums[(h, "bank")][:, c % 2 * H : (c % 2 + 1) * H]
+                    elif h == 1:
+                        f_sums[(h, c)] = spare_bank(c)[:]
+                    else:
+                        f_sums[(h, c)] = bank("g1" if c < 2 else "g2", 2)[:, 0:H]
                 nc.tensor.matmul_mx(
-                    out=f_banks[(h, c)][:],
+                    out=f_sums[(h, c)],
                     lhsT=a_codes[:, g, P * c : P * (c + 1)].bitcast(FP8X4),
                     lhsT_scale=a_scales[:, g, P * c : P * (c + 1)],
-                    rhs=c_codes[h * GROUPS + g][:].bitcast(FP8X4),
-                    rhs_scale=c_scales[h * GROUPS + g][:],
+                    rhs=c_codes[(h, g)][:].bitcast(FP8X4),
+                    rhs_scale=c_scales[(h, g)][:],
                     start=(g == 0),
                     stop=(g == GROUPS - 1),
                 )
 
-        def rescale(h, c, on_vector=False):
-            means[(h, c)] = work.tile([P, W], F32, name="means", bufs=4)
-            if on_vector:
+        def rescale(h, c, engine):
+            means[(h, c)] = work.tile([P, CHUNKS[h][1]], F32, name="means", bufs=4)
+            if engine == "v":
                 nc.vector.tensor_scalar(
                     out=means[(h, c)][:],
-                    in0=f_banks[(h, c)][:],
+                    in0=f_sums[(h, c)],
                     scalar1=gain_col[:, c : c + 1],
                     scalar2=prior_col[:, c : c + 1],
                     op0=ALU.mult,
@@ -238,27 +307,29 @@ def tile_gp_product_kernel_mean_f7_kernel(
             else:
                 nc.scalar.activation(
                     out=means[(h, c)][:],
-                    in_=f_banks[(h, c)][:],
+                    in_=f_sums[(h, c)],
                     func=ACT.Identity,
                     scale=gain_col[:, c : c + 1],
                     bias=prior_col[:, c : c + 1],
                 )
 
-        def turn_mean(h, c):
-            turned[(h, c)] = spare_bank(2 + c % 2) if h == 0 else bank("g1" if c % 2 == 0 else "g2", 2)
-            for r in range(W // P):
-                cols = slice(P * r, P * (r + 1))
-                nc.tensor.transpose(turned[(h, c)][:, cols], means[(h, c)][:, cols], ident[:])
+        def turn_mean(h, cs, b):
+            turned[(h, cs[0])] = spare_bank(b)
+            for r in range(CHUNKS[h][1] // P):
+                for place, c in enumerate(cs):
+                    col = (r * len(cs) + place) * P
+                    nc.tensor.transpose(
+                        turned[(h, cs[0])][:, col : col + P], means[(h, c)][:, P * r : P * (r + 1)], ident[:]
+                    )
 
-        def store_mean(h, c, on_vector=False):
-            rows = work.tile([P, W], F32, name="rows", bufs=4)
-            if on_vector:
-                nc.vector.tensor_copy(out=rows[:], in_=turned[(h, c)][:])
-            else:
-                nc.scalar.copy(out=rows[:], in_=turned[(h, c)][:])
+        def store_mean(h, cs, engine):
+            row0, width = CHUNKS[h]
+            n = width * len(cs)
+            rows = work.tile([P, n], F32, name="rows", bufs=4)
+            copy_out(engine, rows[:], turned[(h, cs[0])][:, 0:n])
             nc.sync.dma_start(
-                out=out[h * W : (h + 1) * W, P * c : P * (c + 1)].rearrange("(r p) c -> p r c", p=P),
-                in_=rows[:].rearrange("p (r c) -> p r c", c=P),
+                out=out[row0 : row0 + width, P * cs[0] : P * (cs[-1] + 1)].rearrange("(r p) c -> p r c", p=P),
+                in_=rows[:].rearrange("p (r c) -> p r c", c=P * len(cs)),
             )
 
         nc.vector.memset(warm[:], 0.0)
@@ -266,32 +337,33 @@ def tile_gp_product_kernel_mean_f7_kernel(
         nc.vector.memset(z_scales[:].rearrange("p g n -> p (g n)").bitcast(I32), 0)
         nc.vector.memset(a_scales[:].rearrange("p g n -> p (g n)").bitcast(I32), 0)
         make_identity(nc, ident[:])
+        load_x(0, 0)
         nc.sync.dma_start(
             out=zs_raw[0:64, 0:2, :].bitcast(I32), in_=z1_scales.rearrange("a q (g m) -> (q g) a m", m=W).bitcast(I32)
         )
         nc.sync.dma_start(
             out=zs_raw[0:64, 2, :].bitcast(I32), in_=z2_scales[0].rearrange("q (g m) -> (q g) m", m=W).bitcast(I32)
         )
-        load_x(0, 0)
-        load_z_codes(slice(0, 2 * W))
         load_x(0, 1)
+        load_z_codes(0)
         load_x(0, 2)
-        nc.scalar.dma_start(out=lz_raw[:], in_=lz.rearrange("(g p t) -> p g t", p=P, t=PACK))
+        nc.sync.dma_start(out=lz_raw[:], in_=lz.rearrange("(g p t) -> p g t", p=P, t=PACK))
         nc.scalar.activation(out=warm_out[:], in_=warm[:], func=ACT.Exp)
         order_z_scales()
         place_z_scales(nc.sync, 0)
-        nc.sync.dma_start(out=lx_all[0][:], in_=lx[0:W].partition_broadcast(P))
+        load_lx(0)
+        load_z_codes(1)
         nc.sync.dma_start(out=amp_raw[:], in_=amp.rearrange("(g p t) -> p g t", p=P, t=PACK))
         nc.gpsimd.tensor_copy(out=lz_col[:], in_=lz_raw[:].rearrange("p g t -> p (g t)"))
         nc.gpsimd.tensor_copy(out=amp_col[:], in_=amp_raw[:].rearrange("p g t -> p (g t)"))
-        load_z_codes(slice(2 * W, 4 * W))
         place_z_scales(nc.sync, 1)
-        load_z_codes(slice(4 * W, 2 * N))
-        for g in range(2, GROUPS):
-            place_z_scales(nc.sync, g)
-        for a in range(Z_PASSES):
-            load_x(1, a)
-        nc.sync.dma_start(out=lx_all[1][:], in_=lx[W : 2 * W].partition_broadcast(P))
+        load_z_codes(2)
+        load_x(1, 0)
+        place_z_scales(nc.sync, 2)
+        load_x(1, 1)
+        place_z_scales(nc.sync, 3)
+        load_x(1, 2)
+        load_lx(1)
         nc.sync.dma_start(
             out=a_codes[:].bitcast(I32), in_=alpha_words.rearrange("g p n t -> p g (n t)").bitcast(I32)
         )
@@ -304,80 +376,107 @@ def tile_gp_product_kernel_mean_f7_kernel(
         )
 
         for a in range(Z_PASSES):
-            turn_x(0, a, 0)
-            turn_x(0, a, 1)
-            group_x(0, a, 0)
-            group_x(0, a, 1)
-        order_z_codes(0, 0)
-        order_z_codes(0, 1)
-        quantize_x(0, 0)
-        order_z_codes(0, 2)
-        quantize_x(0, 1)
-        order_z_codes(1, 0)
-        quantize_x(0, 2)
-        products(0)
+            load_x(2, a)
+        load_lx(2)
 
-        tensor_extra, scalar_extra, vector_extra = {}, {}, {}
+        for a in range(Z_PASSES):
+            turn_x(0, a, 0, a)
+            group_x(0, a, 0, "s")
+        order_z_codes(0, 0)
+        quantize_x(0, 0)
+        order_z_codes(0, 1)
+        quantize_x(0, 1)
+        order_z_codes(0, 2)
+        quantize_x(0, 2)
+        order_z_codes(1, 0)
+
+        tensor_extra, scalar_extra, gpsimd_extra, vector_mid, vector_end = {}, {}, {}, {}, {}
 
         def at(table, step, fn, *args):
             table.setdefault(step, []).append((fn, args))
 
+        def on(engine, step, fn, *args):
+            if engine == "f":
+                at(gpsimd_extra, step, fn, *args, "s")
+            else:
+                at(vector_mid if engine == "v" else scalar_extra, step, fn, *args, engine)
+
+        def run(table, step):
+            for fn, args in table.get(step, []):
+                fn(*args)
+
         for g in range(1, GROUPS):
             for a in range(Z_PASSES):
                 if (g, a) != (1, 0):
-                    at(vector_extra, 4 * g - 5 + a, order_z_codes, g, a)
-        for a in range(Z_PASSES):
-            for pair in range(2):
-                step = 1 + 4 * a + 2 * pair
-                at(tensor_extra, step, turn_x, 1, a, pair)
-                at(scalar_extra, step + 1, group_x, 1, a, pair)
-            at(vector_extra, 6 + 4 * a, quantize_x, 1, a)
-        last = HALVES * GROUPS - 1
-        for u in range(last):
-            split = W - SCALAR_COLS[u]
-            mid = split + SCALAR_COLS[u] // 2
-            at(vector_extra, 4 * u + 6, group_kernel, u, 0, split, True)
-            at(scalar_extra, 4 * u + 6, group_kernel, u, split, mid, False)
-            at(scalar_extra, 4 * u + 7, group_kernel, u, mid, W, False)
-            at(vector_extra, 4 * u + 8, quantize_kernel, u)
-        at(vector_extra, 16, nc.vector.tensor_copy, gain_col[:], gain_raw[:, :, 0])
-        at(vector_extra, 16, nc.vector.tensor_copy, prior_col[:], prior_raw[:, :, 0])
+                    at(vector_mid, g - 1, order_z_codes, g, a)
+        x_moves = [(1, a, pair) for a in range(Z_PASSES) for pair in range(2)] + [(2, a, 0) for a in range(Z_PASSES)]
+        for n, step in enumerate(X_STEPS):
+            h, a, pair = x_moves[n]
+            at(tensor_extra, step, turn_x, h, a, pair, (3 + n) % 4)
+            on(X_ON[n], step, group_x, h, a, pair)
+            if h == 2 or pair == 1:
+                at(vector_end, step + (h == 2), quantize_x, h, a)
+        halves = [(0, g, 0, 2 + g) for g in range(GROUPS)]
+        halves += [(1, g, half, 7 + 2 * g + half) for g in range(GROUPS) for half in range(2)][:-1]
+        halves += [(2, g, 0, 14 + g) for g in range(2)]
+        for h, g, half, step in halves:
+            at(gpsimd_extra, step, group_kernel, h, g, half, 0, G_COLS[step - 2], "g")
+            on(REST_ON[step - 2], step, group_kernel, h, g, half, G_COLS[step - 2], H)
+            if Q_LATE[step - 2] == "1":
+                at(vector_mid, step + 1, quantize_kernel, h, g, half)
+            else:
+                at(vector_end, step, quantize_kernel, h, g, half)
+        on(FULL_ON[0], 13, group_kernel, 1, 3, 1, 0, H)
+        at(vector_end, 13, quantize_kernel, 1, 3, 1)
+        on(FULL_ON[1], 16, group_kernel, 2, 2, 0, 0, H)
+        at(vector_end, 16, quantize_kernel, 2, 2, 0)
+        at(gpsimd_extra, 4, nc.gpsimd.tensor_copy, gain_col[:], gain_raw[:, :, 0])
+        at(gpsimd_extra, 4, nc.gpsimd.tensor_copy, prior_col[:], prior_raw[:, :, 0])
         for c in range(C_TILES):
-            at(tensor_extra, 21 + 2 * c, mean_passes, 0, c, range(GROUPS))
-            at(scalar_extra, 22 + 2 * c, rescale, 0, c)
-            at(tensor_extra, 23 + 2 * c, turn_mean, 0, c)
-            at(scalar_extra, 24 + 2 * c, store_mean, 0, c)
-        for c, step in enumerate((29, 29, 30, 31)):
-            at(tensor_extra, step, mean_passes, 1, c, range(2))
+            at(tensor_extra, 6 + c // 2, mean_passes, 0, c, range(GROUPS))
+            on(EPI_A[c], 6 + c // 2, rescale, 0, c)
+        for pair in range(2):
+            at(tensor_extra, 7 + pair, turn_mean, 0, (2 * pair, 2 * pair + 1), 2 + pair)
+            on(EPI_A[4 + pair], 7 + pair, store_mean, 0, (2 * pair, 2 * pair + 1))
         for c in range(C_TILES):
-            at(tensor_extra, 33, mean_passes, 1, c, range(2, 3))
+            for g, step in enumerate((10, 11, 13, 14)):
+                at(tensor_extra, step, mean_passes, 1, c, range(g, g + 1))
+            on(EPI_B[c], 14 + c // 2, rescale, 1, c)
+            at(tensor_extra, 15 + c // 2, turn_mean, 1, (c,), c)
+            on(EPI_B[4 + c], 15 + c // 2, store_mean, 1, (c,))
+        for c in range(C_TILES):
+            at(tensor_extra, 16, mean_passes, 2, c, range(2))
 
-        for s in range(TILES + 2):
-            if s + 1 < TILES:
-                products(s + 1)
-            for fn, args in tensor_extra.get(s, []):
-                fn(*args)
-            if 1 <= s <= TILES:
-                exponential(s - 1)
-            if s < TILES:
-                square(s)
-                exponent(s)
-            for fn, args in vector_extra.get(s, []):
-                fn(*args)
-            for fn, args in scalar_extra.get(s, []):
-                fn(*args)
-            if s >= 2:
-                kernel_values(s - 2)
+        for s in range(STEPS + 1):
+            now = [k for k in (2 * s, 2 * s + 1) if k < 2 * STEPS]
+            earlier = [k for k in (2 * s - 2, 2 * s - 1) if k >= 0]
+            for k in now:
+                product_1(k)
+            for k in now:
+                product_2(k)
+            run(tensor_extra, s)
+            run(gpsimd_extra, s)
+            for k in earlier:
+                exponential(k)
+            for k in now:
+                square(k)
+                exponent(k)
+            run(scalar_extra, s)
+            run(vector_mid, s)
+            for k in earlier:
+                kernel_values(k)
+            run(vector_end, s)
 
-        split = W - SCALAR_COLS[last]
-        group_kernel(last, split, W, False)
-        group_kernel(last, 0, split, True)
-        quantize_kernel(last)
         for c in range(C_TILES):
-            mean_passes(1, c, range(GROUPS - 1, GROUPS))
+            mean_passes(2, c, range(2, 3))
+        group_kernel(2, 3, 0, TAIL_SPLIT, H, "s")
+        group_kernel(2, 3, 0, 0, TAIL_SPLIT, "v")
+        quantize_kernel(2, 3, 0)
         for c in range(C_TILES):
-            rescale(1, c, on_vector=(c % 2 == 1))
+            mean_passes(2, c, range(3, 4))
         for c in range(C_TILES):
-            turn_mean(1, c)
+            rescale(2, c, "sv"[c % 2])
         for c in range(C_TILES):
-            store_mean(1, c, on_vector=(c % 2 == 1))
+            turn_mean(2, (c,), c)
+        for c in range(C_TILES):
+            store_mean(2, (c,), "sv"[c % 2])

from contextlib import ExitStack

import concourse.mybir as mybir
from concourse.masks import make_identity

M, D, E, N, C = 1024, 1024, 512, 2048, 512
FLOPS = 2 * M * N * (D + E) + 2 * M * N * C

F32 = mybir.dt.float32
BF16 = mybir.dt.bfloat16
I32 = mybir.dt.int32
U32 = mybir.dt.uint32
U8 = mybir.dt.uint8
FP8X4 = mybir.dt.float8_e4m3fn_x4
FP4X4 = mybir.dt.float4_e2m1fn_x4
ALU = mybir.AluOpType
ACT = mybir.ActivationFunctionType

P = 128
PACK = 4
W = 512
H = W // 2
GROUPS = N // W
Z_PASSES = 3
C_TILES = C // P
CHUNKS = ((0, H), (H, W), (H + W, H))
STEPS = 16
REST_ON = "ssfvxvvvssvsvvs"
X_ON = "ssssssssv"
EPI_A = "ssssss"
EPI_B = "sssssvsv"
Q_LATE = "000000000000000"
X_STEPS = (1, 1, 2, 2, 3, 3, 4, 5, 9)
G_COLS = (160, 160, 160, 160, 160, 160, 160, 160, 160, 160, 160, 160, 160, 160, 160)
FULL_ON = "vs"
TAIL_SPLIT = 176


def tile_gp_product_kernel_mean_f7_kernel(
    tc, x1, x2, z1_words, z1_scales, z2_words, z2_scales, alpha_words, alpha_scales, lx, lz, amp, gain, prior, out
):
    nc = tc.nc
    with ExitStack() as ctx:
        keep = ctx.enter_context(tc.tile_pool(name="keep", bufs=1))
        work = ctx.enter_context(tc.tile_pool(name="work", bufs=2))
        psum = ctx.enter_context(tc.psum_pool(name="psum", bufs=1))
        ctx.enter_context(tc.manual_schedule())

        ident = keep.tile([P, P], F32, name="ident")
        warm = keep.tile([P, 1], F32, name="warm")
        warm_out = keep.tile([P, 1], F32, name="warm_out")
        z_parts = [
            keep.tile([P, Z_PASSES, 2 * W * n], U8, name="z_part%d" % g, align_bytes=64) for g, n in enumerate((1, 1, 2))
        ]
        z_raw = [z_parts[0][:], z_parts[1][:], z_parts[2][:, :, 0 : 2 * W], z_parts[2][:, :, 2 * W : 4 * W]]
        zs_raw = keep.tile([P, Z_PASSES, W], U8, name="zs_raw", align_bytes=64)
        zs_ordered = keep.tile([P, Z_PASSES * W], U8, name="zs_ordered", align_bytes=64)
        z_codes = [keep.tile([P, Z_PASSES, 2 * W], U8, name="z_codes%d" % g, align_bytes=64) for g in range(GROUPS)]
        z_scales = keep.tile([P, GROUPS, Z_PASSES * W], U8, name="z_scales", align_bytes=64)
        a_codes = keep.tile([P, GROUPS, C], U32, name="a_codes", align_bytes=64)
        a_scales = keep.tile([P, GROUPS, C], U8, name="a_scales", align_bytes=64)
        x_rows, x_codes, x_scales, c_codes, c_scales, lx_all = {}, {}, {}, {}, {}, {}
        for h, (row0, width) in enumerate(CHUNKS):
            lx_all[h] = keep.tile([P, width], BF16, name="lx_all%d" % h)
            for a in range(Z_PASSES):
                x_rows[(h, a)] = keep.tile([P, width // P, W], BF16, name="x_rows%d_%d" % (h, a), align_bytes=64)
                x_codes[(h, a)] = keep.tile([P, width], U32, name="x_codes%d_%d" % (h, a), align_bytes=64)
                x_scales[(h, a)] = keep.tile([P, width], U8, name="x_scales%d_%d" % (h, a), align_bytes=64)
            for g in range(GROUPS):
                c_codes[(h, g)] = keep.tile([P, width], U32, name="c_codes%d_%d" % (h, g), align_bytes=64)
                c_scales[(h, g)] = keep.tile([P, width], U8, name="c_scales%d_%d" % (h, g), align_bytes=64)
        lz_raw = keep.tile([P, GROUPS, PACK], BF16, name="lz_raw")
        amp_raw = keep.tile([P, GROUPS, PACK], BF16, name="amp_raw")
        lz_col = keep.tile([P, GROUPS * PACK], F32, name="lz_col")
        amp_col = keep.tile([P, GROUPS * PACK], F32, name="amp_col")
        gain_raw = keep.tile([P, C_TILES, 2], BF16, name="gain_raw")
        prior_raw = keep.tile([P, C_TILES, 2], BF16, name="prior_raw")
        gain_col = keep.tile([P, C_TILES], F32, name="gain_col")
        prior_col = keep.tile([P, C_TILES], F32, name="prior_col")

        def bank(tag, bufs=1):
            return psum.tile([P, W], F32, name=tag, tag=tag, bufs=bufs)

        def spare_bank(b):
            return bank("spare%d" % b)

        def load_z_codes(g):
            cols = slice(2 * W * g, 2 * W * g + z_parts[g].shape[2])
            nc.sync.dma_start(
                out=z_parts[g][:, 0:2, :].bitcast(I32), in_=z1_words[:, :, cols].rearrange("g p n -> p g n").bitcast(I32)
            )
            nc.sync.dma_start(out=z_parts[g][:, 2, :].bitcast(I32), in_=z2_words[0, :, cols].bitcast(I32))

        def load_x(h, a):
            row0, width = CHUNKS[h]
            src = x1[:, a * W : (a + 1) * W] if a < 2 else x2
            nc.sync.dma_start(
                out=x_rows[(h, a)][:], in_=src[row0 : row0 + width, :].rearrange("(c p) k -> p c k", p=P)
            )

        def load_lx(h):
            row0, width = CHUNKS[h]
            nc.sync.dma_start(out=lx_all[h][:], in_=lx[row0 : row0 + width].partition_broadcast(P))

        def load_scale_rows(queue, plane, rows):
            for q in range(4):
                queue.dma_start(
                    out=plane[32 * q : 32 * q + 4].bitcast(I32),
                    in_=rows[:, 4 * q : 4 * q + 4, :].rearrange("g r n -> r g n").bitcast(I32),
                )

        def order_z_codes(g, a):
            nc.vector.tensor_copy(
                out=z_codes[g][:, a, :].rearrange("p (t m b) -> p t m b", t=PACK, b=2),
                in_=z_raw[g][:, a, :].rearrange("p (m t b) -> p t m b", t=PACK, b=2),
            )

        def order_z_scales():
            nc.vector.tensor_copy(
                out=zs_ordered[:].rearrange("p (a t m) -> p t a m", a=Z_PASSES, t=PACK),
                in_=zs_raw[:].rearrange("p a (m t) -> p t a m", t=PACK),
            )

        def place_z_scales(queue, g):
            for q in range(4):
                queue.dma_start(
                    out=z_scales[32 * q : 32 * q + 4, g, :].bitcast(I32),
                    in_=zs_ordered[16 * q + g : 16 * (q + 1) : 4, :].bitcast(I32),
                )

        x_banks = {}
        x_grouped = {}

        def turn_x(h, a, pair, b):
            xt = spare_bank(b)
            x_banks[(h, a, pair)] = xt
            for c in range(2):
                words = x_rows[(h, a)][:, 2 * pair + c, :].bitcast(F32)
                for u in range(2):
                    col = (2 * c + u) * P
                    nc.tensor.transpose(xt[:, col : col + P], words[:, u : W // 2 : 2], ident[:])

        def copy_out(engine, dst, src):
            if engine == "v":
                nc.vector.tensor_copy(out=dst, in_=src)
            else:
                nc.scalar.copy(out=dst, in_=src)

        def group_x(h, a, pair, engine):
            if pair == 0:
                x_grouped[(h, a)] = work.tile([P, PACK * CHUNKS[h][1]], BF16, name="x_grouped", align_bytes=64, bufs=3)
            dst = x_grouped[(h, a)][:].bitcast(F32)[:, pair * W : (pair + 1) * W]
            copy_out(
                engine,
                dst.rearrange("p (c r u) -> p c r u", c=2, u=2),
                x_banks[(h, a, pair)][:].rearrange("p (c u r) -> p c r u", c=2, u=2),
            )

        def quantize_x(h, a):
            nc.vector.quantize_mx(
                out=x_codes[(h, a)][:].bitcast(FP8X4), scales=x_scales[(h, a)][:], in_=x_grouped[(h, a)][:]
            )

        slots = []
        for h, (row0, width) in enumerate(CHUNKS):
            per_bank = W // width
            for g in range(GROUPS):
                for t in range(0, PACK, per_bank):
                    slots.append((h, g, list(range(t, t + per_bank))))

        g1, g2, arg, rbf, poly, kern, kern_grouped = {}, {}, {}, {}, {}, {}, {}

        def z_pass(dst, h, g, t, a, cols, start, stop):
            nc.tensor.matmul_mx(
                out=dst,
                lhsT=z_codes[g][:, a, 2 * P * t : 2 * P * (t + 1)].bitcast(FP4X4),
                lhsT_scale=z_scales[:, g, W * a + P * t : W * a + P * (t + 1)],
                rhs=x_codes[(h, a)][:, cols].bitcast(FP8X4),
                rhs_scale=x_scales[(h, a)][:, cols],
                start=start,
                stop=stop,
            )

        def product_1(k):
            h, g, ts = slots[k]
            width = CHUNKS[h][1]
            n = W if width == W else P
            g1[k] = bank("g1", 2)
            for place, t in enumerate(ts):
                for lo in range(0, width, n):
                    dst = g1[k][:, place * width + lo : place * width + lo + n]
                    z_pass(dst, h, g, t, 0, slice(lo, lo + n), True, False)
                    z_pass(dst, h, g, t, 1, slice(lo, lo + n), False, True)

        def product_2(k):
            h, g, ts = slots[k]
            width = CHUNKS[h][1]
            g2[k] = bank("g2", 2)
            for place, t in enumerate(ts):
                z_pass(g2[k][:, place * width : (place + 1) * width], h, g, t, 2, slice(0, width), True, True)

        def exponent(k):
            h, g, ts = slots[k]
            width = CHUNKS[h][1]
            arg[k] = work.tile([P, W], F32, name="arg", bufs=4)
            for place, t in enumerate(ts):
                cols = slice(place * width, (place + 1) * width)
                nc.vector.scalar_tensor_tensor(
                    out=arg[k][:, cols],
                    in0=g1[k][:, cols],
                    scalar=lz_col[:, PACK * g + t : PACK * g + t + 1],
                    in1=lx_all[h][:],
                    op0=ALU.subtract,
                    op1=ALU.subtract,
                )

        def exponential(k):
            rbf[k] = work.tile([P, W], F32, name="rbf", bufs=4)
            nc.scalar.activation(out=rbf[k][:], in_=arg[k][:], func=ACT.Exp)

        def square(k):
            h, g, ts = slots[k]
            if h == 1 and g > 0 and ts[0] == 1:
                poly[k] = work.tile([P, W], F32, name="paced", tag="paced%d" % (g % 2), align_bytes=64, bufs=1)
            else:
                poly[k] = work.tile([P, W], F32, name="poly", bufs=4)
            nc.scalar.activation(out=poly[k][:], in_=g2[k][:], func=ACT.Square, bias=1.0)

        def kernel_values(k):
            h, g, ts = slots[k]
            width = CHUNKS[h][1]
            if ts[0] == 0:
                kern[(h, g)] = work.tile([P, PACK, width], BF16, name="kern", align_bytes=64, bufs=3)
            for place, t in enumerate(ts):
                cols = slice(place * width, (place + 1) * width)
                nc.vector.scalar_tensor_tensor(
                    out=kern[(h, g)][:, t, :],
                    in0=rbf[k][:, cols],
                    scalar=amp_col[:, PACK * g + t : PACK * g + t + 1],
                    in1=poly[k][:, cols],
                    op0=ALU.mult,
                    op1=ALU.mult,
                )

        def group_kernel(h, g, half, lo, hi, engine):
            if (h, g, half) not in kern_grouped:
                if half == 1 and g < GROUPS - 1:
                    tag = "paced%d" % ((g + 1) % 2)
                else:
                    tag = "kern_grouped%d_%d" % (half, g % 2)
                kern_grouped[(h, g, half)] = work.tile(
                    [P, H, PACK], BF16, name="kern_grouped", tag=tag, align_bytes=64, bufs=1
                )
            dst = kern_grouped[(h, g, half)][:, lo:hi, :]
            src = kern[(h, g)][:, :, half * H + lo : half * H + hi]
            if engine == "g":
                nc.gpsimd.tensor_scalar(
                    out=dst, in0=src.rearrange("p t i -> p i t"), scalar1=1.0, scalar2=0.0, op0=ALU.mult, op1=ALU.add
                )
            else:
                copy_out(
                    engine, dst.rearrange("p (c i) t -> p c t i", i=4), src.rearrange("p t (c i) -> p c t i", i=4)
                )

        def quantize_kernel(h, g, half):
            cols = slice(half * H, (half + 1) * H)
            nc.vector.quantize_mx(
                out=c_codes[(h, g)][:, cols].bitcast(FP8X4),
                scales=c_scales[(h, g)][:, cols],
                in_=kern_grouped[(h, g, half)][:].rearrange("p i t -> p (i t)"),
            )

        f_sums, means, turned = {}, {}, {}

        def mean_passes(h, c, groups):
            for g in groups:
                if g == 0:
                    if h == 0:
                        if c % 2 == 0:
                            f_sums[(h, "bank")] = spare_bank(c // 2)
                        f_sums[(h, c)] = f_sums[(h, "bank")][:, c % 2 * H : (c % 2 + 1) * H]
                    elif h == 1:
                        f_sums[(h, c)] = spare_bank(c)[:]
                    else:
                        f_sums[(h, c)] = bank("g1" if c < 2 else "g2", 2)[:, 0:H]
                nc.tensor.matmul_mx(
                    out=f_sums[(h, c)],
                    lhsT=a_codes[:, g, P * c : P * (c + 1)].bitcast(FP8X4),
                    lhsT_scale=a_scales[:, g, P * c : P * (c + 1)],
                    rhs=c_codes[(h, g)][:].bitcast(FP8X4),
                    rhs_scale=c_scales[(h, g)][:],
                    start=(g == 0),
                    stop=(g == GROUPS - 1),
                )

        def rescale(h, c, engine):
            means[(h, c)] = work.tile([P, CHUNKS[h][1]], F32, name="means", bufs=4)
            if engine == "v":
                nc.vector.tensor_scalar(
                    out=means[(h, c)][:],
                    in0=f_sums[(h, c)],
                    scalar1=gain_col[:, c : c + 1],
                    scalar2=prior_col[:, c : c + 1],
                    op0=ALU.mult,
                    op1=ALU.add,
                )
            else:
                nc.scalar.activation(
                    out=means[(h, c)][:],
                    in_=f_sums[(h, c)],
                    func=ACT.Identity,
                    scale=gain_col[:, c : c + 1],
                    bias=prior_col[:, c : c + 1],
                )

        def turn_mean(h, cs, b):
            turned[(h, cs[0])] = spare_bank(b)
            for r in range(CHUNKS[h][1] // P):
                for place, c in enumerate(cs):
                    col = (r * len(cs) + place) * P
                    nc.tensor.transpose(
                        turned[(h, cs[0])][:, col : col + P], means[(h, c)][:, P * r : P * (r + 1)], ident[:]
                    )

        def store_mean(h, cs, engine):
            row0, width = CHUNKS[h]
            n = width * len(cs)
            rows = work.tile([P, n], F32, name="rows", bufs=4)
            copy_out(engine, rows[:], turned[(h, cs[0])][:, 0:n])
            nc.sync.dma_start(
                out=out[row0 : row0 + width, P * cs[0] : P * (cs[-1] + 1)].rearrange("(r p) c -> p r c", p=P),
                in_=rows[:].rearrange("p (r c) -> p r c", c=P * len(cs)),
            )

        nc.vector.memset(warm[:], 0.0)
        nc.vector.memset(zs_raw[64:P].rearrange("p a n -> p (a n)").bitcast(I32), 0)
        nc.vector.memset(z_scales[:].rearrange("p g n -> p (g n)").bitcast(I32), 0)
        nc.vector.memset(a_scales[:].rearrange("p g n -> p (g n)").bitcast(I32), 0)
        make_identity(nc, ident[:])
        load_x(0, 0)
        nc.sync.dma_start(
            out=zs_raw[0:64, 0:2, :].bitcast(I32), in_=z1_scales.rearrange("a q (g m) -> (q g) a m", m=W).bitcast(I32)
        )
        nc.sync.dma_start(
            out=zs_raw[0:64, 2, :].bitcast(I32), in_=z2_scales[0].rearrange("q (g m) -> (q g) m", m=W).bitcast(I32)
        )
        load_x(0, 1)
        load_z_codes(0)
        load_x(0, 2)
        nc.sync.dma_start(out=lz_raw[:], in_=lz.rearrange("(g p t) -> p g t", p=P, t=PACK))
        nc.scalar.activation(out=warm_out[:], in_=warm[:], func=ACT.Exp)
        order_z_scales()
        place_z_scales(nc.sync, 0)
        load_lx(0)
        load_z_codes(1)
        nc.sync.dma_start(out=amp_raw[:], in_=amp.rearrange("(g p t) -> p g t", p=P, t=PACK))
        nc.gpsimd.tensor_copy(out=lz_col[:], in_=lz_raw[:].rearrange("p g t -> p (g t)"))
        nc.gpsimd.tensor_copy(out=amp_col[:], in_=amp_raw[:].rearrange("p g t -> p (g t)"))
        place_z_scales(nc.sync, 1)
        load_z_codes(2)
        load_x(1, 0)
        place_z_scales(nc.sync, 2)
        load_x(1, 1)
        place_z_scales(nc.sync, 3)
        load_x(1, 2)
        load_lx(1)
        nc.sync.dma_start(
            out=a_codes[:].bitcast(I32), in_=alpha_words.rearrange("g p n t -> p g (n t)").bitcast(I32)
        )
        load_scale_rows(nc.sync, a_scales, alpha_scales)
        nc.sync.dma_start(
            out=gain_raw[:, :, 0], in_=gain.rearrange("(c p) -> p c", p=P), allow_slow_non_contiguous=True
        )
        nc.sync.dma_start(
            out=prior_raw[:, :, 0], in_=prior.rearrange("(c p) -> p c", p=P), allow_slow_non_contiguous=True
        )

        for a in range(Z_PASSES):
            load_x(2, a)
        load_lx(2)

        for a in range(Z_PASSES):
            turn_x(0, a, 0, a)
            group_x(0, a, 0, "s")
        order_z_codes(0, 0)
        quantize_x(0, 0)
        order_z_codes(0, 1)
        quantize_x(0, 1)
        order_z_codes(0, 2)
        quantize_x(0, 2)
        order_z_codes(1, 0)

        tensor_extra, scalar_extra, gpsimd_extra, vector_mid, vector_end = {}, {}, {}, {}, {}

        def at(table, step, fn, *args):
            table.setdefault(step, []).append((fn, args))

        def on(engine, step, fn, *args):
            if engine == "f":
                at(gpsimd_extra, step, fn, *args, "s")
            else:
                at(vector_mid if engine == "v" else scalar_extra, step, fn, *args, engine)

        def run(table, step):
            for fn, args in table.get(step, []):
                fn(*args)

        for g in range(1, GROUPS):
            for a in range(Z_PASSES):
                if (g, a) != (1, 0):
                    at(vector_mid, g - 1, order_z_codes, g, a)
        x_moves = [(1, a, pair) for a in range(Z_PASSES) for pair in range(2)] + [(2, a, 0) for a in range(Z_PASSES)]
        for n, step in enumerate(X_STEPS):
            h, a, pair = x_moves[n]
            at(tensor_extra, step, turn_x, h, a, pair, (3 + n) % 4)
            on(X_ON[n], step, group_x, h, a, pair)
            if h == 2 or pair == 1:
                at(vector_end, step + (h == 2), quantize_x, h, a)
        halves = [(0, g, 0, 2 + g) for g in range(GROUPS)]
        halves += [(1, g, half, 7 + 2 * g + half) for g in range(GROUPS) for half in range(2)][:-1]
        halves += [(2, g, 0, 14 + g) for g in range(2)]
        for h, g, half, step in halves:
            at(gpsimd_extra, step, group_kernel, h, g, half, 0, G_COLS[step - 2], "g")
            on(REST_ON[step - 2], step, group_kernel, h, g, half, G_COLS[step - 2], H)
            if Q_LATE[step - 2] == "1":
                at(vector_mid, step + 1, quantize_kernel, h, g, half)
            else:
                at(vector_end, step, quantize_kernel, h, g, half)
        on(FULL_ON[0], 13, group_kernel, 1, 3, 1, 0, H)
        at(vector_end, 13, quantize_kernel, 1, 3, 1)
        on(FULL_ON[1], 16, group_kernel, 2, 2, 0, 0, H)
        at(vector_end, 16, quantize_kernel, 2, 2, 0)
        at(gpsimd_extra, 4, nc.gpsimd.tensor_copy, gain_col[:], gain_raw[:, :, 0])
        at(gpsimd_extra, 4, nc.gpsimd.tensor_copy, prior_col[:], prior_raw[:, :, 0])
        for c in range(C_TILES):
            at(tensor_extra, 6 + c // 2, mean_passes, 0, c, range(GROUPS))
            on(EPI_A[c], 6 + c // 2, rescale, 0, c)
        for pair in range(2):
            at(tensor_extra, 7 + pair, turn_mean, 0, (2 * pair, 2 * pair + 1), 2 + pair)
            on(EPI_A[4 + pair], 7 + pair, store_mean, 0, (2 * pair, 2 * pair + 1))
        for c in range(C_TILES):
            for g, step in enumerate((10, 11, 13, 14)):
                at(tensor_extra, step, mean_passes, 1, c, range(g, g + 1))
            on(EPI_B[c], 14 + c // 2, rescale, 1, c)
            at(tensor_extra, 15 + c // 2, turn_mean, 1, (c,), c)
            on(EPI_B[4 + c], 15 + c // 2, store_mean, 1, (c,))
        for c in range(C_TILES):
            at(tensor_extra, 16, mean_passes, 2, c, range(2))

        for s in range(STEPS + 1):
            now = [k for k in (2 * s, 2 * s + 1) if k < 2 * STEPS]
            earlier = [k for k in (2 * s - 2, 2 * s - 1) if k >= 0]
            for k in now:
                product_1(k)
            for k in now:
                product_2(k)
            run(tensor_extra, s)
            run(gpsimd_extra, s)
            for k in earlier:
                exponential(k)
            for k in now:
                square(k)
                exponent(k)
            run(scalar_extra, s)
            run(vector_mid, s)
            for k in earlier:
                kernel_values(k)
            run(vector_end, s)

        for c in range(C_TILES):
            mean_passes(2, c, range(2, 3))
        group_kernel(2, 3, 0, TAIL_SPLIT, H, "s")
        group_kernel(2, 3, 0, 0, TAIL_SPLIT, "v")
        quantize_kernel(2, 3, 0)
        for c in range(C_TILES):
            mean_passes(2, c, range(3, 4))
        for c in range(C_TILES):
            rescale(2, c, "sv"[c % 2])
        for c in range(C_TILES):
            turn_mean(2, (c,), c)
        for c in range(C_TILES):
            store_mean(2, (c,), "sv"[c % 2])
